import numpy as np
import ml_dtypes


def mxq(x, axis, fmt="e4m3"):
    dtype, down = {"e4m3": (ml_dtypes.float8_e4m3fn, 7), "e5m2": (ml_dtypes.float8_e5m2, 14)}[fmt]
    v = np.moveaxis(np.asarray(x, np.float32).astype(ml_dtypes.bfloat16).astype(np.float64), axis, -1)
    blocks = v.reshape(v.shape[:-1] + (-1, 32))
    amax = np.abs(blocks).max(-1, keepdims=True)
    byte = np.maximum(np.where(amax > 0, np.frexp(amax)[1] - 1 + 127, 0) - down, 1)
    scale = np.exp2(byte - 127.0)
    codes = (blocks / scale).astype(np.float32).astype(dtype).astype(np.float64)
    return np.moveaxis((codes * scale).reshape(v.shape), -1, axis)


WIDE = False


def mx_kscale(k):
    if not WIDE:
        return np.ones(k)
    levels = np.array([10, -10, 5, -5, 0])
    if k % 512:
        return np.exp2(np.random.permutation(np.resize(levels, k // 32))).repeat(32)
    a = np.empty((k // 512, 16))
    for p in range(k // 512):
        a[p, :8] = np.random.permutation(np.resize(levels, 8))
        for g in range(8):
            far = levels[np.abs(levels - a[p, g]) >= 10]
            a[p, g + 8] = far[np.random.randint(len(far))]
    return np.exp2(a.ravel()).repeat(32)


def f64(x):
    return np.asarray(x).astype(np.float64)


def striped(idx):
    return np.tile(idx.reshape(-1, 16).T, (8, 1)).astype(np.uint16)


def unstriped(offs):
    return offs[:16].T.reshape(-1).astype(np.int64)


def pack_weight(w):
    k, n = w.shape
    w = f64(np.asarray(w, np.float32).astype(ml_dtypes.bfloat16)).reshape(k // 32, 32, n)
    amax = np.abs(w).max(1)
    byte = np.clip(np.where(amax > 0, np.frexp(amax)[1] - 1 + 127 - 7, 1), 1, 254)
    scaled = (w * np.exp2(127.0 - byte)[:, None, :]).reshape(k, n).astype(np.float32)
    words = np.ascontiguousarray(scaled.reshape(k // 512, 128, 4, n).transpose(0, 1, 3, 2)).astype(ml_dtypes.float8_e4m3fn).view(np.uint8)
    return words, np.ascontiguousarray(byte.astype(np.uint8).reshape(k // 512, 16, n))


def unpack_weight(words, scales):
    g, p, n, _ = words.shape
    vals = np.ascontiguousarray(words).view(ml_dtypes.float8_e4m3fn).astype(np.float64) * np.repeat(np.exp2(scales.astype(np.float64) - 127.0), 8, axis=1)[..., None]
    return vals.transpose(0, 1, 3, 2).reshape(g * 512, n)


def sigmoid(v):
    return 1.0 / (1.0 + np.exp(-np.maximum(v, -700.0)))


K, T, S, N, H, W, G = 512, 1024, 512, 256, 512, 2048, 2048


def setup_inputs():
    n = np.random.standard_normal
    s = mx_kscale(K)[:, None]
    u = mx_kscale(H)
    packed_xT = pack_weight(n((K, T)) * s)
    packed_eT = pack_weight(n((K, W)) * s)
    packed_dT = pack_weight(n((K, G)) * s)
    return {
        "x_words": packed_xT[0],
        "x_scales": packed_xT[1],
        "w1": (n((K, H)) / np.sqrt(K) / s).astype(np.float32),
        "e_words": packed_eT[0],
        "e_scales": packed_eT[1],
        "w2": (n((K, H)) / np.sqrt(K) / s).astype(np.float32),
        "d_words": packed_dT[0],
        "d_scales": packed_dT[1],
        "w3": (n((K, H)) / np.sqrt(K) / s).astype(np.float32),
        "unit": (np.random.uniform(0.6, 1.4, (H, 1)) * u[:, None]).astype(np.float32),
        "w4": (n((H, N)) / np.sqrt(H) / u[:, None]).astype(np.float32),
        "offs": striped(np.random.permutation(T)[:S]),
        "nbc": striped(np.random.permutation(W)[:S]),
        "cnt": striped(np.random.permutation(G)[:S]),
        "al1": striped(np.random.permutation(S)),
        "alc": striped(np.random.permutation(S)),
        "al2": striped(np.random.permutation(S)),
    }


def reference(x_words, x_scales, w1, e_words, e_scales, w2, d_words, d_scales, w3, unit, w4, offs, nbc, cnt, al1, alc, al2):
    xq = unpack_weight(x_words, x_scales)[:, unstriped(offs)]
    y = mxq(f64(w1), 0, "e4m3").T @ xq
    e_nbc = unpack_weight(e_words, e_scales)[:, unstriped(nbc)]
    ye = mxq(f64(w2), 0, "e4m3").T @ e_nbc
    e1 = ye[:, unstriped(al1)]
    gate_ = sigmoid(y * e1)
    d_cnt = unpack_weight(d_words, d_scales)[:, unstriped(cnt)]
    yd = mxq(f64(w3), 0, "e4m3").T @ d_cnt
    d1 = yd[:, unstriped(alc)]
    fus = y + gate_ * d1
    e2 = ye[:, unstriped(al2)]
    hid = f64(unit) * (fus - (0.5 * e2))
    return mxq(f64(w4), 0, "e4m3").T @ mxq(hid, 0, "e4m3")

@@ -1,0 +1,188 @@
+from contextlib import ExitStack
+
+import concourse.mybir as mybir
+
+F32 = mybir.dt.float32
+BF16 = mybir.dt.bfloat16
+I32 = mybir.dt.int32
+U32 = mybir.dt.uint32
+U16 = mybir.dt.uint16
+U8 = mybir.dt.uint8
+FP8X4 = mybir.dt.float8_e4m3fn_x4
+ALU = mybir.AluOpType
+ACT = mybir.ActivationFunctionType
+
+P = 128
+PACK = 4
+K, H, S, N = 512, 512, 512, 256
+SPARE = 16
+PIECES = ((0, 256), (256, 128), (384, 128))
+
+FLOPS = 2 * K * H * S * 3 + 2 * H * N * S
+
+
+def tile_picked_yretroc_con_p_kernel(
+    tc, x_words, x_scales, w1, e_words, e_scales, w2, d_words, d_scales, w3, unit, w4,
+    offs, nbc, cnt, al1, alc, al2, out,
+):
+    nc = tc.nc
+    with ExitStack() as ctx:
+        keep = ctx.enter_context(tc.tile_pool(name="keep", bufs=1))
+        psum = ctx.enter_context(tc.psum_pool(name="psum", bufs=1))
+
+        def load_list(src, name):
+            t = keep.tile([P, S // 16], U16, name=name)
+            nc.sync.dma_start(t[:], src)
+            return t
+
+        def load_words(src, name):
+            t = keep.tile([P, src.shape[2]], I32, name=name, align_bytes=64)
+            nc.sync.dma_start(t[:], src[0].rearrange("p n r -> p (n r)").bitcast(I32))
+            return t
+
+        def load_scales(src, name, clear, queue):
+            t = keep.tile([P, src.shape[2]], U8, name=name, align_bytes=64)
+            clear.memset(t[:].bitcast(I32), 0)
+            for q in range(4):
+                queue.dma_start(t[32 * q : 32 * q + 4, :].bitcast(I32), src[0, 4 * q : 4 * q + 4, :].bitcast(I32))
+            return t
+
+        def load_weight_half(w, h, name):
+            t = keep.tile([P, PACK, H // 2], F32, name=name)
+            nc.sync.dma_start(t[:], w.rearrange("(p j) c -> p j c", j=PACK)[:, :, h * (H // 2) : (h + 1) * (H // 2)])
+            return t
+
+        def pick(words, scales, idx, name):
+            pw = keep.tile([P, S], U32, name=name + "_w", align_bytes=64)
+            ps = keep.tile([P, S], U8, name=name + "_s", align_bytes=64)
+            nc.vector.tensor_copy(ps[:], scales[:].indirect(idx[:]))
+            nc.vector.tensor_copy(pw[:], words[:].bitcast(U32).indirect(idx[:]))
+            return pw, ps
+
+        def deal_half(copy, raw, h, dealt):
+            m = P // 2
+            copy(
+                out=dealt[:].rearrange("p (t m j) -> p m j t", t=PACK, j=PACK)[:, h * m : (h + 1) * m],
+                in_=raw[:].rearrange("p j (m t) -> p m j t", t=PACK),
+            )
+
+        def quantize(src, name, calls):
+            width = src.shape[1] // PACK
+            codes = keep.tile([P, width], U32, name=name + "_c", align_bytes=64)
+            scales = keep.tile([P, width], U8, name=name + "_b", align_bytes=64)
+            step = width // calls
+            for c in range(0, width, step):
+                nc.vector.quantize_mx(
+                    out=codes[:, c : c + step].bitcast(FP8X4),
+                    scales=scales[:, c : c + step],
+                    in_=src[:, PACK * c : PACK * (c + step)],
+                )
+            return codes, scales
+
+        def product(dst, wq, t, xq):
+            cols = slice(t * P, (t + 1) * P)
+            nc.tensor.matmul_mx(
+                out=dst, lhsT=wq[0][:, cols].bitcast(FP8X4), lhsT_scale=wq[1][:, cols],
+                rhs=xq[0][:].bitcast(FP8X4), rhs_scale=xq[1][:], start=True, stop=True,
+            )
+
+        def fetch(dst, window, idx, c0, width):
+            nc.scalar.activation(dst[:, c0 : c0 + width], window[:].indirect(idx[:, c0 // 16 : (c0 + width) // 16]), ACT.Copy)
+
+        nbc_t = load_list(nbc, "nbc_t")
+        offs_t = load_list(offs, "offs_t")
+        al1_t = load_list(al1, "al1_t")
+        es = load_scales(e_scales, "es", nc.vector, nc.gpsimd)
+        xs = load_scales(x_scales, "xs", nc.vector, nc.gpsimd)
+        ds = load_scales(d_scales, "ds", nc.vector, nc.gpsimd)
+        w2_raw = [load_weight_half(w2, h, "w2_raw%d" % h) for h in range(2)]
+        ew = load_words(e_words, "ew")
+        xw = load_words(x_words, "xw")
+        w1_raw = [load_weight_half(w1, h, "w1_raw%d" % h) for h in range(2)]
+        al2_t = load_list(al2, "al2_t")
+        cnt_t = load_list(cnt, "cnt_t")
+        dw = load_words(d_words, "dw")
+        w3_raw = [load_weight_half(w3, h, "w3_raw%d" % h) for h in range(2)]
+        unit_t = keep.tile([P, PACK], F32, name="unit_t")
+        nc.sync.dma_start(unit_t[:], unit.rearrange("(p t) o -> p (t o)", t=PACK))
+        alc_t = load_list(alc, "alc_t")
+        w4_raw = keep.tile([P, PACK, N], F32, name="w4_raw")
+        nc.sync.dma_start(w4_raw[:], w4.rearrange("(p j) c -> p j c", j=PACK))
+
+        w2_dealt = keep.tile([P, PACK * H], BF16, name="w2_dealt", align_bytes=64)
+        deal_half(nc.scalar.copy, w2_raw[0], 0, w2_dealt)
+        deal_half(nc.vector.tensor_copy, w2_raw[1], 1, w2_dealt)
+        w2q = quantize(w2_dealt, "w2q", 1)
+        eq = pick(ew, es, nbc_t, "eq")
+        ye, e1, e2 = [], [], []
+        for t in range(PACK):
+            ye.append(keep.tile([P, S + SPARE], F32, name="ye%d" % t))
+            nc.vector.memset(ye[t][:, S:], 0.0)
+        for t in range(PACK):
+            bank = psum.tile([P, S], F32, name="ye_bank%d" % t, tag="r%d" % t)
+            product(bank[:], w2q, t, eq)
+            nc.scalar.copy(out=ye[t][:, :S], in_=bank[:])
+            e1.append(keep.tile([P, S], F32, name="e1_%d" % t))
+            fetch(e1[t], ye[t], al1_t, 0, S)
+
+        xq = pick(xw, xs, offs_t, "xq")
+        w1_dealt = keep.tile([P, PACK * H], BF16, name="w1_dealt", align_bytes=64)
+        for h in range(2):
+            deal_half(nc.vector.tensor_copy, w1_raw[h], h, w1_dealt)
+        w1q = quantize(w1_dealt, "w1q", 2)
+        y, z, gate = [], [], []
+        for t in range(PACK):
+            y.append(psum.tile([P, S], F32, name="y%d" % t))
+            product(y[t][:], w1q, t, xq)
+            z.append(keep.tile([P, S], F32, name="z%d" % t))
+            nc.vector.tensor_tensor(z[t][:], y[t][:], e1[t][:], ALU.mult)
+
+        for t in range(PACK):
+            e2.append(keep.tile([P, S], F32, name="e2_%d" % t))
+            fetch(e2[t], ye[t], al2_t, 0, S)
+            gate.append(keep.tile([P, S], F32, name="gate%d" % t))
+            nc.scalar.activation(gate[t][:], z[t][:], ACT.Sigmoid)
+
+        dq = pick(dw, ds, cnt_t, "dq")
+        w3_dealt = keep.tile([P, PACK * H], BF16, name="w3_dealt", align_bytes=64)
+        for h in range(2):
+            deal_half(nc.vector.tensor_copy, w3_raw[h], h, w3_dealt)
+        w3q = quantize(w3_dealt, "w3q", 2)
+        yd, base = [], []
+        for t in range(PACK):
+            bank = psum.tile([P, S], F32, name="yd_bank%d" % t, tag="r%d" % t)
+            product(bank[:], w3q, t, dq)
+            yd.append(keep.tile([P, S], F32, name="yd%d" % t))
+            nc.scalar.activation(yd[t][:], bank[:], ACT.Copy, scale=unit_t[:, t : t + 1])
+            base.append(keep.tile([P, S], F32, name="base%d" % t))
+            nc.vector.scalar_tensor_tensor(base[t][:], e2[t][:], -0.5, y[t][:], ALU.mult, ALU.add)
+
+        w4_grouped = keep.tile([P, PACK * N], BF16, name="w4_grouped", align_bytes=64)
+        nc.vector.tensor_copy(
+            out=w4_grouped[:].rearrange("p (c i j) -> p c j i", i=4, j=PACK),
+            in_=w4_raw[:].rearrange("p j (c i) -> p c j i", i=4),
+        )
+        w4q = quantize(w4_grouped, "w4q", 1)
+
+        out_v = out.rearrange("(m p) j -> p m j", p=P)
+        for n, (c0, width) in enumerate(PIECES):
+            cols = slice(c0, c0 + width)
+            hid = keep.tile([P, PACK, width], F32, name="hid%d" % n)
+            for t in range(PACK):
+                d1 = keep.tile([P, width], F32, name="d1_%d_%d" % (n, t))
+                nc.scalar.activation(d1[:], yd[t][:].indirect(alc_t[:, c0 // 16 : (c0 + width) // 16]), ACT.Copy)
+                gated = keep.tile([P, width], F32, name="gated%d_%d" % (n, t))
+                nc.vector.tensor_tensor(gated[:], d1[:], gate[t][:, cols], ALU.mult)
+                nc.vector.scalar_tensor_tensor(hid[:, t, :], base[t][:, cols], unit_t[:, t : t + 1], gated[:], ALU.mult, ALU.add)
+            grouped = keep.tile([P, PACK * width], BF16, name="grouped%d" % n, align_bytes=64)
+            nc.vector.tensor_copy(
+                out=grouped[:].rearrange("p (c i t) -> p c t i", i=4, t=PACK),
+                in_=hid[:].rearrange("p t (c i) -> p c t i", i=4),
+            )
+            hq = quantize(grouped, "hq%d" % n, 1)
+            bank = psum.tile([P, 2, width], F32, name="out_bank%d" % n, tag="r%d" % n)
+            for m in range(2):
+                product(bank[:, m, :], w4q, m, hq)
+            res = keep.tile([P, 2, width], F32, name="res%d" % n)
+            nc.scalar.copy(out=res[:], in_=bank[:])
+            nc.sync.dma_start(out_v[:, :, cols], res[:])

@@ -16,6 +16,7 @@ P = 128
 PACK = 4
 K, H, S, N = 512, 512, 512, 256
 SPARE = 16
+TINY = 2.0 ** -120
 PIECES = ((0, 256), (256, 128), (384, 128))
 
 FLOPS = 2 * K * H * S * 3 + 2 * H * N * S
@@ -40,11 +41,16 @@ def tile_picked_yretroc_con_p_kernel(
             nc.sync.dma_start(t[:], src[0].rearrange("p n r -> p (n r)").bitcast(I32))
             return t
 
-        def load_scales(src, name, clear, queue):
+        def load_scales(src, name):
             t = keep.tile([P, src.shape[2]], U8, name=name, align_bytes=64)
-            clear.memset(t[:].bitcast(I32), 0)
+            nc.vector.memset(t[:].bitcast(I32), 0)
             for q in range(4):
-                queue.dma_start(t[32 * q : 32 * q + 4, :].bitcast(I32), src[0, 4 * q : 4 * q + 4, :].bitcast(I32))
+                nc.sync.dma_start(t[32 * q : 32 * q + 4, :].bitcast(I32), src[0, 4 * q : 4 * q + 4, :].bitcast(I32))
+            return t
+
+        def load_weight(w, name):
+            t = keep.tile([P, PACK, w.shape[1]], F32, name=name, align_bytes=64)
+            nc.sync.dma_start(t[:], w.rearrange("(p j) c -> p j c", j=PACK))
             return t
 
         def load_weight_half(w, h, name):
@@ -52,18 +58,23 @@ def tile_picked_yretroc_con_p_kernel(
             nc.sync.dma_start(t[:], w.rearrange("(p j) c -> p j c", j=PACK)[:, :, h * (H // 2) : (h + 1) * (H // 2)])
             return t
 
-        def pick(words, scales, idx, name):
+        def deal_half(copy, raw, dealt, h):
+            copy(
+                out=dealt[:].rearrange("p (t m j) -> p m j t", t=PACK, j=PACK)[:, h * P // 2 : (h + 1) * P // 2],
+                in_=raw[:].rearrange("p j (m t) -> p m j t", t=PACK),
+            )
+
+        def pick(words, scales, idx, name, slot):
             pw = keep.tile([P, S], U32, name=name + "_w", align_bytes=64)
-            ps = keep.tile([P, S], U8, name=name + "_s", align_bytes=64)
+            ps = keep.tile([P, S], U8, name=name + "_s", tag=slot, align_bytes=64)
             nc.vector.tensor_copy(ps[:], scales[:].indirect(idx[:]))
             nc.vector.tensor_copy(pw[:], words[:].bitcast(U32).indirect(idx[:]))
             return pw, ps
 
-        def deal_half(copy, raw, h, dealt):
-            m = P // 2
+        def deal(copy, raw, dealt, m0, m1):
             copy(
-                out=dealt[:].rearrange("p (t m j) -> p m j t", t=PACK, j=PACK)[:, h * m : (h + 1) * m],
-                in_=raw[:].rearrange("p j (m t) -> p m j t", t=PACK),
+                out=dealt[:].rearrange("p (t m j) -> p m j t", t=PACK, j=PACK)[:, m0:m1],
+                in_=raw[:].rearrange("p j (m t) -> p m j t", t=PACK)[:, m0:m1],
             )
 
         def quantize(src, name, calls):
@@ -87,33 +98,47 @@ def tile_picked_yretroc_con_p_kernel(
             )
 
         def fetch(dst, window, idx, c0, width):
-            nc.scalar.activation(dst[:, c0 : c0 + width], window[:].indirect(idx[:, c0 // 16 : (c0 + width) // 16]), ACT.Copy)
+            nc.scalar.activation(dst, window[:].indirect(idx[:, c0 // 16 : (c0 + width) // 16]), ACT.Copy)
 
-        nbc_t = load_list(nbc, "nbc_t")
-        offs_t = load_list(offs, "offs_t")
-        al1_t = load_list(al1, "al1_t")
-        es = load_scales(e_scales, "es", nc.vector, nc.gpsimd)
-        xs = load_scales(x_scales, "xs", nc.vector, nc.gpsimd)
-        ds = load_scales(d_scales, "ds", nc.vector, nc.gpsimd)
-        w2_raw = [load_weight_half(w2, h, "w2_raw%d" % h) for h in range(2)]
-        ew = load_words(e_words, "ew")
-        xw = load_words(x_words, "xw")
-        w1_raw = [load_weight_half(w1, h, "w1_raw%d" % h) for h in range(2)]
-        al2_t = load_list(al2, "al2_t")
-        cnt_t = load_list(cnt, "cnt_t")
-        dw = load_words(d_words, "dw")
-        w3_raw = [load_weight_half(w3, h, "w3_raw%d" % h) for h in range(2)]
+        def vfetch(dst, window, idx, c0, width):
+            nc.vector.tensor_copy(dst, window[:].indirect(idx[:, c0 // 16 : (c0 + width) // 16]))
+
         unit_t = keep.tile([P, PACK], F32, name="unit_t")
-        nc.sync.dma_start(unit_t[:], unit.rearrange("(p t) o -> p (t o)", t=PACK))
+        nc.gpsimd.dma_start(unit_t[:], unit.rearrange("(p t) o -> p (t o)", t=PACK))
+        w2_raw = [load_weight_half(w2, 0, "w2_raw0")]
+        nbc_t = load_list(nbc, "nbc_t")
+        es = load_scales(e_scales, "es")
+        w2_raw.append(load_weight_half(w2, 1, "w2_raw1"))
+        ew = load_words(e_words, "ew")
+        al1_t = load_list(al1, "al1_t")
+        w1_raw = [load_weight_half(w1, h, "w1_raw%d" % h) for h in range(2)]
+        offs_t = load_list(offs, "offs_t")
+        xs = load_scales(x_scales, "xs")
+        xw = load_words(x_words, "xw")
+        dw = load_words(d_words, "dw")
+        cnt_t = load_list(cnt, "cnt_t")
+        ds = load_scales(d_scales, "ds")
+        al2_t = load_list(al2, "al2_t")
+        w3_raw = load_weight(w3, "w3_raw")
         alc_t = load_list(alc, "alc_t")
-        w4_raw = keep.tile([P, PACK, N], F32, name="w4_raw")
-        nc.sync.dma_start(w4_raw[:], w4.rearrange("(p j) c -> p j c", j=PACK))
+        w4_raw = load_weight(w4, "w4_raw")
+
+        half_unit = keep.tile([P, PACK], F32, name="half_unit")
+        neg_half_unit = keep.tile([P, PACK], F32, name="neg_half_unit")
+        square = keep.tile([P, PACK], F32, name="square")
+        vanishes = keep.tile([P, PACK], F32, name="vanishes")
+        safe = keep.tile([P, PACK], F32, name="safe")
+        nc.gpsimd.tensor_scalar(neg_half_unit[:], unit_t[:], -0.5, 0.0, ALU.mult, ALU.add)
+        nc.gpsimd.tensor_scalar(half_unit[:], unit_t[:], 0.5, 0.0, ALU.mult, ALU.add)
+        nc.gpsimd.tensor_tensor(square[:], unit_t[:], unit_t[:], ALU.mult)
+        nc.gpsimd.tensor_scalar(vanishes[:], square[:], TINY, None, ALU.is_lt)
+        nc.gpsimd.tensor_tensor(safe[:], vanishes[:], unit_t[:], ALU.subtract)
 
         w2_dealt = keep.tile([P, PACK * H], BF16, name="w2_dealt", align_bytes=64)
-        deal_half(nc.scalar.copy, w2_raw[0], 0, w2_dealt)
-        deal_half(nc.vector.tensor_copy, w2_raw[1], 1, w2_dealt)
+        deal_half(nc.scalar.copy, w2_raw[0], w2_dealt, 0)
+        deal_half(nc.vector.tensor_copy, w2_raw[1], w2_dealt, 1)
         w2q = quantize(w2_dealt, "w2q", 1)
-        eq = pick(ew, es, nbc_t, "eq")
+        eq = pick(ew, es, nbc_t, "eq", "eq_s")
         ye, e1, e2 = [], [], []
         for t in range(PACK):
             ye.append(keep.tile([P, S + SPARE], F32, name="ye%d" % t))
@@ -121,42 +146,49 @@ def tile_picked_yretroc_con_p_kernel(
         for t in range(PACK):
             bank = psum.tile([P, S], F32, name="ye_bank%d" % t, tag="r%d" % t)
             product(bank[:], w2q, t, eq)
-            nc.scalar.copy(out=ye[t][:, :S], in_=bank[:])
+            nc.scalar.activation(ye[t][:, :S], bank[:], ACT.Copy, scale=neg_half_unit[:, t : t + 1])
             e1.append(keep.tile([P, S], F32, name="e1_%d" % t))
-            fetch(e1[t], ye[t], al1_t, 0, S)
+            fetch(e1[t][:], ye[t], al1_t, 0, S)
 
-        xq = pick(xw, xs, offs_t, "xq")
         w1_dealt = keep.tile([P, PACK * H], BF16, name="w1_dealt", align_bytes=64)
         for h in range(2):
-            deal_half(nc.vector.tensor_copy, w1_raw[h], h, w1_dealt)
-        w1q = quantize(w1_dealt, "w1q", 2)
-        y, z, gate = [], [], []
+            deal_half(nc.vector.tensor_copy, w1_raw[h], w1_dealt, h)
+        w1q = quantize(w1_dealt, "w1q", 1)
+        xq = pick(xw, xs, offs_t, "xq", "ew")
+        undo = keep.tile([P, PACK], F32, name="undo", tag="w1_dealt", align_bytes=64)
+        nc.vector.reciprocal(undo[:], safe[:])
+        y = []
         for t in range(PACK):
             y.append(psum.tile([P, S], F32, name="y%d" % t))
             product(y[t][:], w1q, t, xq)
-            z.append(keep.tile([P, S], F32, name="z%d" % t))
-            nc.vector.tensor_tensor(z[t][:], y[t][:], e1[t][:], ALU.mult)
 
+        gate = keep.tile([P, PACK, S], F32, name="gate")
+
+        def make_gate(pair, slot, align):
+            z = keep.tile([P, 2, S], F32, name="z%d" % pair, tag=slot, align_bytes=align)
+            for i in range(2):
+                t = 2 * pair + i
+                nc.vector.tensor_tensor(z[:, i, :], y[t][:], e1[t][:], ALU.mult)
+                nc.scalar.activation(gate[:, t, :], z[:, i, :], ACT.Tanh, scale=undo[:, t : t + 1])
+
+        dq = pick(dw, ds, cnt_t, "dq", "xw")
+        make_gate(0, "dw", 64)
+        w3_dealt = keep.tile([P, PACK * H], BF16, name="w3_dealt", align_bytes=64)
+        deal(nc.vector.tensor_copy, w3_raw, w3_dealt, 0, P)
+        w3q = quantize(w3_dealt, "w3q", 1)
         for t in range(PACK):
             e2.append(keep.tile([P, S], F32, name="e2_%d" % t))
-            fetch(e2[t], ye[t], al2_t, 0, S)
-            gate.append(keep.tile([P, S], F32, name="gate%d" % t))
-            nc.scalar.activation(gate[t][:], z[t][:], ACT.Sigmoid)
-
-        dq = pick(dw, ds, cnt_t, "dq")
-        w3_dealt = keep.tile([P, PACK * H], BF16, name="w3_dealt", align_bytes=64)
-        for h in range(2):
-            deal_half(nc.vector.tensor_copy, w3_raw[h], h, w3_dealt)
-        w3q = quantize(w3_dealt, "w3q", 2)
-        yd, base = [], []
+            fetch(e2[t][:], ye[t], al2_t, 0, S)
+        make_gate(1, "w3_raw", 64)
+        yd = []
         for t in range(PACK):
             bank = psum.tile([P, S], F32, name="yd_bank%d" % t, tag="r%d" % t)
             product(bank[:], w3q, t, dq)
             yd.append(keep.tile([P, S], F32, name="yd%d" % t))
-            nc.scalar.activation(yd[t][:], bank[:], ACT.Copy, scale=unit_t[:, t : t + 1])
-            base.append(keep.tile([P, S], F32, name="base%d" % t))
-            nc.vector.scalar_tensor_tensor(base[t][:], e2[t][:], -0.5, y[t][:], ALU.mult, ALU.add)
-
+            if t < 1:
+                nc.scalar.activation(yd[t][:], bank[:], ACT.Copy, scale=half_unit[:, t : t + 1])
+            else:
+                nc.vector.tensor_scalar(yd[t][:], bank[:], half_unit[:, t : t + 1], None, ALU.mult)
         w4_grouped = keep.tile([P, PACK * N], BF16, name="w4_grouped", align_bytes=64)
         nc.vector.tensor_copy(
             out=w4_grouped[:].rearrange("p (c i j) -> p c j i", i=4, j=PACK),
@@ -164,20 +196,28 @@ def tile_picked_yretroc_con_p_kernel(
         )
         w4q = quantize(w4_grouped, "w4q", 1)
 
+        base = keep.tile([P, PACK, S], F32, name="base", tag="w3_dealt", align_bytes=64)
+        for t in range(PACK):
+            nc.vector.scalar_tensor_tensor(base[:, t, :], y[t][:], unit_t[:, t : t + 1], e2[t][:], ALU.mult, ALU.add)
+
+        fetched = keep.tile([P, PACK * S], F32, name="fetched", tag="w3_raw", align_bytes=64)
         out_v = out.rearrange("(m p) j -> p m j", p=P)
         for n, (c0, width) in enumerate(PIECES):
             cols = slice(c0, c0 + width)
-            hid = keep.tile([P, PACK, width], F32, name="hid%d" % n)
+            d1 = fetched[:, PACK * c0 : PACK * (c0 + width)].rearrange("p (t w) -> p t w", t=PACK)
+            gated = keep.tile([P, PACK, width], F32, name="gated%d" % n)
             for t in range(PACK):
-                d1 = keep.tile([P, width], F32, name="d1_%d_%d" % (n, t))
-                nc.scalar.activation(d1[:], yd[t][:].indirect(alc_t[:, c0 // 16 : (c0 + width) // 16]), ACT.Copy)
-                gated = keep.tile([P, width], F32, name="gated%d_%d" % (n, t))
-                nc.vector.tensor_tensor(gated[:], d1[:], gate[t][:, cols], ALU.mult)
-                nc.vector.scalar_tensor_tensor(hid[:, t, :], base[t][:, cols], unit_t[:, t : t + 1], gated[:], ALU.mult, ALU.add)
+                fetch(d1[:, t, :], yd[t], alc_t, c0, width)
+                if t % 2 == 1:
+                    nc.vector.scalar_tensor_tensor(
+                        gated[:, t - 1 : t + 1, :], gate[:, t - 1 : t + 1, cols], 1.0, d1[:, t - 1 : t + 1, :], ALU.add, ALU.mult
+                    )
             grouped = keep.tile([P, PACK * width], BF16, name="grouped%d" % n, align_bytes=64)
-            nc.vector.tensor_copy(
-                out=grouped[:].rearrange("p (c i t) -> p c t i", i=4, t=PACK),
-                in_=hid[:].rearrange("p t (c i) -> p c t i", i=4),
+            nc.vector.tensor_tensor(
+                grouped[:].rearrange("p (c i t) -> p c t i", i=4, t=PACK),
+                gated[:].rearrange("p t (c i) -> p c t i", i=4),
+                base[:, :, cols].rearrange("p t (c i) -> p c t i", i=4),
+                ALU.add,
             )
             hq = quantize(grouped, "hq%d" % n, 1)
             bank = psum.tile([P, 2, width], F32, name="out_bank%d" % n, tag="r%d" % n)

from contextlib import ExitStack

import concourse.mybir as mybir

F32 = mybir.dt.float32
BF16 = mybir.dt.bfloat16
I32 = mybir.dt.int32
U32 = mybir.dt.uint32
U16 = mybir.dt.uint16
U8 = mybir.dt.uint8
FP8X4 = mybir.dt.float8_e4m3fn_x4
ALU = mybir.AluOpType
ACT = mybir.ActivationFunctionType

P = 128
PACK = 4
K, H, S, N = 512, 512, 512, 256
SPARE = 16
TINY = 2.0 ** -120
PIECES = ((0, 256), (256, 128), (384, 128))

FLOPS = 2 * K * H * S * 3 + 2 * H * N * S


def tile_picked_yretroc_con_p_kernel(
    tc, x_words, x_scales, w1, e_words, e_scales, w2, d_words, d_scales, w3, unit, w4,
    offs, nbc, cnt, al1, alc, al2, out,
):
    nc = tc.nc
    with ExitStack() as ctx:
        keep = ctx.enter_context(tc.tile_pool(name="keep", bufs=1))
        psum = ctx.enter_context(tc.psum_pool(name="psum", bufs=1))

        def load_list(src, name):
            t = keep.tile([P, S // 16], U16, name=name)
            nc.sync.dma_start(t[:], src)
            return t

        def load_words(src, name):
            t = keep.tile([P, src.shape[2]], I32, name=name, align_bytes=64)
            nc.sync.dma_start(t[:], src[0].rearrange("p n r -> p (n r)").bitcast(I32))
            return t

        def load_scales(src, name):
            t = keep.tile([P, src.shape[2]], U8, name=name, align_bytes=64)
            nc.vector.memset(t[:].bitcast(I32), 0)
            for q in range(4):
                nc.sync.dma_start(t[32 * q : 32 * q + 4, :].bitcast(I32), src[0, 4 * q : 4 * q + 4, :].bitcast(I32))
            return t

        def load_weight(w, name):
            t = keep.tile([P, PACK, w.shape[1]], F32, name=name, align_bytes=64)
            nc.sync.dma_start(t[:], w.rearrange("(p j) c -> p j c", j=PACK))
            return t

        def load_weight_half(w, h, name):
            t = keep.tile([P, PACK, H // 2], F32, name=name)
            nc.sync.dma_start(t[:], w.rearrange("(p j) c -> p j c", j=PACK)[:, :, h * (H // 2) : (h + 1) * (H // 2)])
            return t

        def deal_half(copy, raw, dealt, h):
            copy(
                out=dealt[:].rearrange("p (t m j) -> p m j t", t=PACK, j=PACK)[:, h * P // 2 : (h + 1) * P // 2],
                in_=raw[:].rearrange("p j (m t) -> p m j t", t=PACK),
            )

        def pick(words, scales, idx, name, slot):
            pw = keep.tile([P, S], U32, name=name + "_w", align_bytes=64)
            ps = keep.tile([P, S], U8, name=name + "_s", tag=slot, align_bytes=64)
            nc.vector.tensor_copy(ps[:], scales[:].indirect(idx[:]))
            nc.vector.tensor_copy(pw[:], words[:].bitcast(U32).indirect(idx[:]))
            return pw, ps

        def deal(copy, raw, dealt, m0, m1):
            copy(
                out=dealt[:].rearrange("p (t m j) -> p m j t", t=PACK, j=PACK)[:, m0:m1],
                in_=raw[:].rearrange("p j (m t) -> p m j t", t=PACK)[:, m0:m1],
            )

        def quantize(src, name, calls):
            width = src.shape[1] // PACK
            codes = keep.tile([P, width], U32, name=name + "_c", align_bytes=64)
            scales = keep.tile([P, width], U8, name=name + "_b", align_bytes=64)
            step = width // calls
            for c in range(0, width, step):
                nc.vector.quantize_mx(
                    out=codes[:, c : c + step].bitcast(FP8X4),
                    scales=scales[:, c : c + step],
                    in_=src[:, PACK * c : PACK * (c + step)],
                )
            return codes, scales

        def product(dst, wq, t, xq):
            cols = slice(t * P, (t + 1) * P)
            nc.tensor.matmul_mx(
                out=dst, lhsT=wq[0][:, cols].bitcast(FP8X4), lhsT_scale=wq[1][:, cols],
                rhs=xq[0][:].bitcast(FP8X4), rhs_scale=xq[1][:], start=True, stop=True,
            )

        def fetch(dst, window, idx, c0, width):
            nc.scalar.activation(dst, window[:].indirect(idx[:, c0 // 16 : (c0 + width) // 16]), ACT.Copy)

        def vfetch(dst, window, idx, c0, width):
            nc.vector.tensor_copy(dst, window[:].indirect(idx[:, c0 // 16 : (c0 + width) // 16]))

        unit_t = keep.tile([P, PACK], F32, name="unit_t")
        nc.gpsimd.dma_start(unit_t[:], unit.rearrange("(p t) o -> p (t o)", t=PACK))
        w2_raw = [load_weight_half(w2, 0, "w2_raw0")]
        nbc_t = load_list(nbc, "nbc_t")
        es = load_scales(e_scales, "es")
        w2_raw.append(load_weight_half(w2, 1, "w2_raw1"))
        ew = load_words(e_words, "ew")
        al1_t = load_list(al1, "al1_t")
        w1_raw = [load_weight_half(w1, h, "w1_raw%d" % h) for h in range(2)]
        offs_t = load_list(offs, "offs_t")
        xs = load_scales(x_scales, "xs")
        xw = load_words(x_words, "xw")
        dw = load_words(d_words, "dw")
        cnt_t = load_list(cnt, "cnt_t")
        ds = load_scales(d_scales, "ds")
        al2_t = load_list(al2, "al2_t")
        w3_raw = load_weight(w3, "w3_raw")
        alc_t = load_list(alc, "alc_t")
        w4_raw = load_weight(w4, "w4_raw")

        half_unit = keep.tile([P, PACK], F32, name="half_unit")
        neg_half_unit = keep.tile([P, PACK], F32, name="neg_half_unit")
        square = keep.tile([P, PACK], F32, name="square")
        vanishes = keep.tile([P, PACK], F32, name="vanishes")
        safe = keep.tile([P, PACK], F32, name="safe")
        nc.gpsimd.tensor_scalar(neg_half_unit[:], unit_t[:], -0.5, 0.0, ALU.mult, ALU.add)
        nc.gpsimd.tensor_scalar(half_unit[:], unit_t[:], 0.5, 0.0, ALU.mult, ALU.add)
        nc.gpsimd.tensor_tensor(square[:], unit_t[:], unit_t[:], ALU.mult)
        nc.gpsimd.tensor_scalar(vanishes[:], square[:], TINY, None, ALU.is_lt)
        nc.gpsimd.tensor_tensor(safe[:], vanishes[:], unit_t[:], ALU.subtract)

        w2_dealt = keep.tile([P, PACK * H], BF16, name="w2_dealt", align_bytes=64)
        deal_half(nc.scalar.copy, w2_raw[0], w2_dealt, 0)
        deal_half(nc.vector.tensor_copy, w2_raw[1], w2_dealt, 1)
        w2q = quantize(w2_dealt, "w2q", 1)
        eq = pick(ew, es, nbc_t, "eq", "eq_s")
        ye, e1, e2 = [], [], []
        for t in range(PACK):
            ye.append(keep.tile([P, S + SPARE], F32, name="ye%d" % t))
            nc.vector.memset(ye[t][:, S:], 0.0)
        for t in range(PACK):
            bank = psum.tile([P, S], F32, name="ye_bank%d" % t, tag="r%d" % t)
            product(bank[:], w2q, t, eq)
            nc.scalar.activation(ye[t][:, :S], bank[:], ACT.Copy, scale=neg_half_unit[:, t : t + 1])
            e1.append(keep.tile([P, S], F32, name="e1_%d" % t))
            fetch(e1[t][:], ye[t], al1_t, 0, S)

        w1_dealt = keep.tile([P, PACK * H], BF16, name="w1_dealt", align_bytes=64)
        for h in range(2):
            deal_half(nc.vector.tensor_copy, w1_raw[h], w1_dealt, h)
        w1q = quantize(w1_dealt, "w1q", 1)
        xq = pick(xw, xs, offs_t, "xq", "ew")
        undo = keep.tile([P, PACK], F32, name="undo", tag="w1_dealt", align_bytes=64)
        nc.vector.reciprocal(undo[:], safe[:])
        y = []
        for t in range(PACK):
            y.append(psum.tile([P, S], F32, name="y%d" % t))
            product(y[t][:], w1q, t, xq)

        gate = keep.tile([P, PACK, S], F32, name="gate")

        def make_gate(pair, slot, align):
            z = keep.tile([P, 2, S], F32, name="z%d" % pair, tag=slot, align_bytes=align)
            for i in range(2):
                t = 2 * pair + i
                nc.vector.tensor_tensor(z[:, i, :], y[t][:], e1[t][:], ALU.mult)
                nc.scalar.activation(gate[:, t, :], z[:, i, :], ACT.Tanh, scale=undo[:, t : t + 1])

        dq = pick(dw, ds, cnt_t, "dq", "xw")
        make_gate(0, "dw", 64)
        w3_dealt = keep.tile([P, PACK * H], BF16, name="w3_dealt", align_bytes=64)
        deal(nc.vector.tensor_copy, w3_raw, w3_dealt, 0, P)
        w3q = quantize(w3_dealt, "w3q", 1)
        for t in range(PACK):
            e2.append(keep.tile([P, S], F32, name="e2_%d" % t))
            fetch(e2[t][:], ye[t], al2_t, 0, S)
        make_gate(1, "w3_raw", 64)
        yd = []
        for t in range(PACK):
            bank = psum.tile([P, S], F32, name="yd_bank%d" % t, tag="r%d" % t)
            product(bank[:], w3q, t, dq)
            yd.append(keep.tile([P, S], F32, name="yd%d" % t))
            if t < 1:
                nc.scalar.activation(yd[t][:], bank[:], ACT.Copy, scale=half_unit[:, t : t + 1])
            else:
                nc.vector.tensor_scalar(yd[t][:], bank[:], half_unit[:, t : t + 1], None, ALU.mult)
        w4_grouped = keep.tile([P, PACK * N], BF16, name="w4_grouped", align_bytes=64)
        nc.vector.tensor_copy(
            out=w4_grouped[:].rearrange("p (c i j) -> p c j i", i=4, j=PACK),
            in_=w4_raw[:].rearrange("p j (c i) -> p c j i", i=4),
        )
        w4q = quantize(w4_grouped, "w4q", 1)

        base = keep.tile([P, PACK, S], F32, name="base", tag="w3_dealt", align_bytes=64)
        for t in range(PACK):
            nc.vector.scalar_tensor_tensor(base[:, t, :], y[t][:], unit_t[:, t : t + 1], e2[t][:], ALU.mult, ALU.add)

        fetched = keep.tile([P, PACK * S], F32, name="fetched", tag="w3_raw", align_bytes=64)
        out_v = out.rearrange("(m p) j -> p m j", p=P)
        for n, (c0, width) in enumerate(PIECES):
            cols = slice(c0, c0 + width)
            d1 = fetched[:, PACK * c0 : PACK * (c0 + width)].rearrange("p (t w) -> p t w", t=PACK)
            gated = keep.tile([P, PACK, width], F32, name="gated%d" % n)
            for t in range(PACK):
                fetch(d1[:, t, :], yd[t], alc_t, c0, width)
                if t % 2 == 1:
                    nc.vector.scalar_tensor_tensor(
                        gated[:, t - 1 : t + 1, :], gate[:, t - 1 : t + 1, cols], 1.0, d1[:, t - 1 : t + 1, :], ALU.add, ALU.mult
                    )
            grouped = keep.tile([P, PACK * width], BF16, name="grouped%d" % n, align_bytes=64)
            nc.vector.tensor_tensor(
                grouped[:].rearrange("p (c i t) -> p c t i", i=4, t=PACK),
                gated[:].rearrange("p t (c i) -> p c t i", i=4),
                base[:, :, cols].rearrange("p t (c i) -> p c t i", i=4),
                ALU.add,
            )
            hq = quantize(grouped, "hq%d" % n, 1)
            bank = psum.tile([P, 2, width], F32, name="out_bank%d" % n, tag="r%d" % n)
            for m in range(2):
                product(bank[:, m, :], w4q, m, hq)
            res = keep.tile([P, 2, width], F32, name="res%d" % n)
            nc.scalar.copy(out=res[:], in_=bank[:])
            nc.sync.dma_start(out_v[:, :, cols], res[:])
